import numpy as np
import ml_dtypes


def mxq(x, axis, fmt="e4m3"):
    dtype, down = {"e4m3": (ml_dtypes.float8_e4m3fn, 7), "e5m2": (ml_dtypes.float8_e5m2, 14)}[fmt]
    v = np.moveaxis(np.asarray(x, np.float32).astype(ml_dtypes.bfloat16).astype(np.float64), axis, -1)
    blocks = v.reshape(v.shape[:-1] + (-1, 32))
    amax = np.abs(blocks).max(-1, keepdims=True)
    byte = np.maximum(np.where(amax > 0, np.frexp(amax)[1] - 1 + 127, 0) - down, 1)
    scale = np.exp2(byte - 127.0)
    codes = (blocks / scale).astype(np.float32).astype(dtype).astype(np.float64)
    return np.moveaxis((codes * scale).reshape(v.shape), -1, axis)


WIDE = False


def mx_kscale(k):
    if not WIDE:
        return np.ones(k)
    levels = np.array([10, -10, 5, -5, 0])
    if k % 512:
        return np.exp2(np.random.permutation(np.resize(levels, k // 32))).repeat(32)
    a = np.empty((k // 512, 16))
    for p in range(k // 512):
        a[p, :8] = np.random.permutation(np.resize(levels, 8))
        for g in range(8):
            far = levels[np.abs(levels - a[p, g]) >= 10]
            a[p, g + 8] = far[np.random.randint(len(far))]
    return np.exp2(a.ravel()).repeat(32)


def f64(x):
    return np.asarray(x).astype(np.float64)


def striped(idx):
    return np.tile(idx.reshape(-1, 16).T, (8, 1)).astype(np.uint16)


def unstriped(offs):
    return offs[:16].T.reshape(-1).astype(np.int64)


def gelu(v):
    return 0.5 * v * (1.0 + np.tanh(np.sqrt(2.0 / np.pi) * (v + 0.044715 * v**3)))


K, T, E, C, N = 2048, 768, 24, 128, 128
TOP = 4


def by_expert(wq, xq):
    return np.concatenate([wq[e].T @ xq[:, e * C:(e + 1) * C] for e in range(E)], axis=1)


def setup_inputs():
    n = np.random.standard_normal
    s = mx_kscale(K)[:, None]
    deal = np.repeat(np.arange(E), C).reshape(TOP, T)[:, np.random.permutation(T)]
    deal = np.take_along_axis(deal, np.argsort(np.random.rand(TOP, T), axis=0), axis=0)
    for _ in range(8):
        s_, t_ = np.random.permutation(T).reshape(2, -1); r = np.random.randint(TOP, size=T // 2); x, y = deal[r, s_].copy(), deal[r, t_].copy()
        ok = ~((deal[:, s_] == y).any(0) | (deal[:, t_] == x).any(0)); deal[r[ok], s_[ok]] = y[ok]; deal[r[ok], t_[ok]] = x[ok]
    order = np.lexsort((np.random.rand(TOP * T), deal.reshape(-1)))
    slot_token = order % T; pos = np.empty(TOP * T, np.int64); pos[order] = np.arange(TOP * T); pos = pos.reshape(TOP, T)
    g = np.random.uniform(0.5, 1.5, (TOP, T)); g = g / g.sum(0)
    w_slot = np.empty(E * C)
    for r in range(TOP): w_slot[pos[r]] = g[r]
    return {
        "xT": (n((K, T)) * s).astype(np.float32),
        "w": (n((E, K, N)) / np.sqrt(K) / s[None]).astype(np.float32),
        "b": (0.3 * n((N, E))).astype(np.float32),
        "gate": np.tile(w_slot, (K, 1)).astype(np.float32),
        "offs": striped(slot_token),
        "pos1": striped(pos[0]),
        "pos2": striped(pos[1]),
        "pos3": striped(pos[2]),
        "pos4": striped(pos[3]),
    }


def reference(xT, w, b, gate, offs, pos1, pos2, pos3, pos4):
    idx = unstriped(offs)
    xq = mxq(f64(gate) * f64(xT)[:, idx], 0, "e4m3")
    y = by_expert(mxq(f64(w), 1, "e4m3"), xq)
    y = gelu(y + np.repeat(f64(b), C, axis=1))
    return y[:, unstriped(pos1)] + y[:, unstriped(pos2)] + y[:, unstriped(pos3)] + y[:, unstriped(pos4)]

@@ -1,0 +1,129 @@
+from contextlib import ExitStack
+
+import concourse.mybir as mybir
+
+K, T, E, C, N = 2048, 768, 24, 128, 128
+TOP = 4
+SLOTS = E * C
+FLOPS = 2 * K * N * SLOTS
+BYTES = 4 * (K * T + E * K * N + N * E + SLOTS + N * T) + 2 * 128 * (SLOTS + TOP * T) // 16
+
+F32 = mybir.dt.float32
+BF16 = mybir.dt.bfloat16
+U32 = mybir.dt.uint32
+U16 = mybir.dt.uint16
+U8 = mybir.dt.uint8
+FP8X4 = mybir.dt.float8_e4m3fn_x4
+MULT = mybir.AluOpType.mult
+ADD = mybir.AluOpType.add
+GELU = mybir.ActivationFunctionType.Gelu_apprx_tanh
+
+P = 128
+PACK = 4
+K_PASS = P * PACK
+PASSES = K // K_PASS
+GROUP = 4
+GROUP_SLOTS = GROUP * C
+GROUPS = E // GROUP
+PER_COL = 16
+LINE = 4
+
+
+def tile_moe_pre_lin_gelu_kernel(tc, xT, w, b, gate, offs, pos1, pos2, pos3, pos4, out):
+    nc = tc.nc
+    steps = [(c, g) for c in range(GROUPS) for g in range(PASSES)]
+    x_rows = xT.rearrange("(g p t) s -> g t p s", p=P, t=PACK)
+
+    with ExitStack() as ctx:
+        keep = ctx.enter_context(tc.tile_pool(name="keep", bufs=1))
+        wload = ctx.enter_context(tc.tile_pool(name="wload", bufs=4))
+        stage = ctx.enter_context(tc.tile_pool(name="stage", bufs=3))
+        psum = ctx.enter_context(tc.psum_pool(name="psum", bufs=2))
+
+        slot_list = keep.tile([P, SLOTS // PER_COL], U16, name="slot_list")
+        pos_lists = [keep.tile([P, T // PER_COL], U16, name="pos_list%d" % r) for r in range(TOP)]
+        planes = [[keep.tile([P, T], F32, name="plane%d_%d" % (g, t)) for t in range(PACK)] for g in range(PASSES)]
+        gates = [keep.tile([P, GROUP_SLOTS], F32, name="gate%d" % c) for c in range(GROUPS)]
+        bias = keep.tile([P, E], F32, name="bias")
+        y = keep.tile([P, SLOTS], F32, name="y")
+
+        w_raw, gathered, x_bf, w_bf, banks = {}, {}, {}, {}, {}
+
+        def load(s):
+            c, g = steps[s]
+            if g == 0:
+                nc.sync.dma_start(out=gates[c][:], in_=gate[0:P, c * GROUP_SLOTS:(c + 1) * GROUP_SLOTS])
+            if c == 0:
+                for t in range(PACK):
+                    nc.sync.dma_start(out=planes[g][t][:], in_=x_rows[g, t])
+            w_raw[s] = wload.tile([P, GROUP, PACK * N], F32, name="w_raw")
+            nc.sync.dma_start(
+                out=w_raw[s][:],
+                in_=w[c * GROUP:(c + 1) * GROUP, g * K_PASS:(g + 1) * K_PASS, :].rearrange("e (p j) n -> p e (j n)", j=PACK))
+
+        def gather(s):
+            c, g = steps[s]
+            cols = GROUP_SLOTS // PER_COL
+            gathered[s] = stage.tile([P, PACK, GROUP_SLOTS], F32, name="gathered")
+            for t in range(PACK):
+                nc.vector.tensor_tensor(gathered[s][:, t, :], planes[g][t][:].indirect(slot_list[:, c * cols:(c + 1) * cols]),
+                                        gates[c][:], MULT)
+
+        def weave(s):
+            w_bf[s] = stage.tile([P, GROUP * N * PACK], BF16, name="w_bf", align_bytes=64)
+            nc.scalar.copy(out=w_bf[s][:].rearrange("p (e c i j) -> p e c j i", e=GROUP, i=LINE, j=PACK),
+                           in_=w_raw[s][:].rearrange("p e (j c i) -> p e c j i", j=PACK, i=LINE))
+            x_bf[s] = stage.tile([P, GROUP_SLOTS * PACK], BF16, name="x_bf", align_bytes=64)
+            nc.scalar.copy(out=x_bf[s][:].rearrange("p (c i t) -> p c t i", i=LINE, t=PACK),
+                           in_=gathered[s][:].rearrange("p t (c i) -> p c t i", i=LINE))
+
+        def quantize(src, name):
+            codes = stage.tile([P, GROUP_SLOTS], U32, name=name + "_codes", align_bytes=64)
+            scales = stage.tile([P, GROUP_SLOTS], U8, name=name + "_scales", align_bytes=64)
+            nc.vector.quantize_mx(out=codes[:].bitcast(FP8X4), scales=scales[:], in_=src[:])
+            return codes, scales
+
+        def multiply(s):
+            c, g = steps[s]
+            w_codes, w_scales = quantize(w_bf[s], "w")
+            x_codes, x_scales = quantize(x_bf[s], "x")
+            for i in range(GROUP):
+                if g == 0:
+                    banks[c, i] = psum.tile([N, C], F32, name="acc%d" % i)
+                cols = slice(i * C, (i + 1) * C)
+                nc.tensor.matmul_mx(out=banks[c, i][:], lhsT=w_codes[:, cols].bitcast(FP8X4), lhsT_scale=w_scales[:, cols],
+                                    rhs=x_codes[:, cols].bitcast(FP8X4), rhs_scale=x_scales[:, cols],
+                                    start=(g == 0), stop=(g == PASSES - 1))
+                if g == PASSES - 1:
+                    e = c * GROUP + i
+                    nc.scalar.activation(out=y[:, e * C:(e + 1) * C], in_=banks[c, i][:], func=GELU, bias=bias[:, e:e + 1])
+
+        nc.sync.dma_start(slot_list[:], offs)
+        load(0)
+        load(1)
+        nc.sync.dma_start(out=bias[:], in_=b)
+        for tile, src in zip(pos_lists, (pos1, pos2, pos3, pos4)):
+            nc.sync.dma_start(tile[:], src)
+        for s in range(len(steps) + 1):
+            if s + 2 < len(steps):
+                load(s + 2)
+            if s < len(steps):
+                gather(s)
+                weave(s)
+            if s >= 1:
+                multiply(s - 1)
+
+        half = T // 2
+        cols = half // PER_COL
+        sums = [None, None]
+        for r in range(TOP):
+            for h in range(2):
+                picked = y[:].indirect(pos_lists[r][:, h * cols:(h + 1) * cols])
+                total = keep.tile([P, half], F32, name="sum%d_%d" % (r, h))
+                if r == 0:
+                    nc.vector.tensor_copy(total[:], picked)
+                else:
+                    nc.vector.tensor_tensor(total[:], picked, sums[h][:], ADD)
+                sums[h] = total
+        nc.sync.dma_start(out=out[:, 0:half], in_=sums[0][:])
+        nc.scalar.dma_start(out=out[:, half:T], in_=sums[1][:])

@@ -22,77 +22,103 @@ P = 128
 PACK = 4
 K_PASS = P * PACK
 PASSES = K // K_PASS
-GROUP = 4
+GROUP = 8
 GROUP_SLOTS = GROUP * C
 GROUPS = E // GROUP
 PER_COL = 16
+WINDOW = GROUP_SLOTS + PER_COL
 LINE = 4
+W_LOAD = 4
+FIRST = 256
 
 
 def tile_moe_pre_lin_gelu_kernel(tc, xT, w, b, gate, offs, pos1, pos2, pos3, pos4, out):
     nc = tc.nc
     steps = [(c, g) for c in range(GROUPS) for g in range(PASSES)]
+    last = len(steps) - 1
     x_rows = xT.rearrange("(g p t) s -> g t p s", p=P, t=PACK)
 
     with ExitStack() as ctx:
         keep = ctx.enter_context(tc.tile_pool(name="keep", bufs=1))
         wload = ctx.enter_context(tc.tile_pool(name="wload", bufs=4))
-        stage = ctx.enter_context(tc.tile_pool(name="stage", bufs=3))
-        psum = ctx.enter_context(tc.psum_pool(name="psum", bufs=2))
+        stage = ctx.enter_context(tc.tile_pool(name="stage", bufs=2))
+        sums = ctx.enter_context(tc.tile_pool(name="sums", bufs=4))
+        psum = ctx.enter_context(tc.psum_pool(name="psum", bufs=1))
 
         slot_list = keep.tile([P, SLOTS // PER_COL], U16, name="slot_list")
         pos_lists = [keep.tile([P, T // PER_COL], U16, name="pos_list%d" % r) for r in range(TOP)]
-        planes = [[keep.tile([P, T], F32, name="plane%d_%d" % (g, t)) for t in range(PACK)] for g in range(PASSES)]
+        planes = [[keep.tile([P, WINDOW], F32, name="plane%d_%d" % (g, t)) for t in range(PACK)] for g in range(PASSES)]
         gates = [keep.tile([P, GROUP_SLOTS], F32, name="gate%d" % c) for c in range(GROUPS)]
         bias = keep.tile([P, E], F32, name="bias")
         y = keep.tile([P, SLOTS], F32, name="y")
 
-        w_raw, gathered, x_bf, w_bf, banks = {}, {}, {}, {}, {}
+        w_raw, w_bf, w_mx, gathered, x_bf, banks = {}, {}, {}, {}, {}, {}
+
+        def pieces(s):
+            return [(0, GROUP)] if s < last else [(0, GROUP // 2), (GROUP // 2, GROUP)]
+
+        def load_gate(c, lo, hi):
+            nc.sync.dma_start(out=gates[c][:, lo:hi], in_=gate[0:P, c * GROUP_SLOTS + lo:c * GROUP_SLOTS + hi])
 
         def load(s):
             c, g = steps[s]
             if g == 0:
-                nc.sync.dma_start(out=gates[c][:], in_=gate[0:P, c * GROUP_SLOTS:(c + 1) * GROUP_SLOTS])
+                load_gate(c, 0, FIRST if s == 0 else GROUP_SLOTS)
             if c == 0:
                 for t in range(PACK):
-                    nc.sync.dma_start(out=planes[g][t][:], in_=x_rows[g, t])
-            w_raw[s] = wload.tile([P, GROUP, PACK * N], F32, name="w_raw")
-            nc.sync.dma_start(
-                out=w_raw[s][:],
-                in_=w[c * GROUP:(c + 1) * GROUP, g * K_PASS:(g + 1) * K_PASS, :].rearrange("e (p j) n -> p e (j n)", j=PACK))
+                    nc.sync.dma_start(out=planes[g][t][:, 0:T], in_=x_rows[g, t])
+                    if s == 0 and t == 0:
+                        load_gate(c, FIRST, GROUP_SLOTS)
+            for h in range(GROUP // W_LOAD):
+                e0 = c * GROUP + h * W_LOAD
+                w_raw[s, h] = wload.tile([P, W_LOAD, PACK * N], F32, name="w_raw")
+                nc.sync.dma_start(
+                    out=w_raw[s, h][:],
+                    in_=w[e0:e0 + W_LOAD, g * K_PASS:(g + 1) * K_PASS, :].rearrange("e (p j) n -> p e (j n)", j=PACK))
 
-        def gather(s):
+        def gather(s, e_lo, e_hi):
             c, g = steps[s]
-            cols = GROUP_SLOTS // PER_COL
-            gathered[s] = stage.tile([P, PACK, GROUP_SLOTS], F32, name="gathered")
+            tile = stage.tile([P, PACK, (e_hi - e_lo) * C], F32, name="gathered" if e_lo == 0 else "gathered_tail")
+            gathered[s, e_lo] = tile
             for t in range(PACK):
-                nc.vector.tensor_tensor(gathered[s][:, t, :], planes[g][t][:].indirect(slot_list[:, c * cols:(c + 1) * cols]),
-                                        gates[c][:], MULT)
+                lo, hi = e_lo * C, e_hi * C
+                cuts = [lo, FIRST, hi] if s == 0 and t == 0 else [lo, hi]
+                for a, z in zip(cuts, cuts[1:]):
+                    offsets = slot_list[:, (c * GROUP_SLOTS + a) // PER_COL:(c * GROUP_SLOTS + z) // PER_COL]
+                    nc.vector.tensor_tensor(tile[:, t, a - lo:z - lo], planes[g][t][:].indirect(offsets), gates[c][:, a:z], MULT)
 
-        def weave(s):
+        def weave_w(s):
             w_bf[s] = stage.tile([P, GROUP * N * PACK], BF16, name="w_bf", align_bytes=64)
-            nc.scalar.copy(out=w_bf[s][:].rearrange("p (e c i j) -> p e c j i", e=GROUP, i=LINE, j=PACK),
-                           in_=w_raw[s][:].rearrange("p e (j c i) -> p e c j i", j=PACK, i=LINE))
-            x_bf[s] = stage.tile([P, GROUP_SLOTS * PACK], BF16, name="x_bf", align_bytes=64)
-            nc.scalar.copy(out=x_bf[s][:].rearrange("p (c i t) -> p c t i", i=LINE, t=PACK),
-                           in_=gathered[s][:].rearrange("p t (c i) -> p c t i", i=LINE))
+            width = W_LOAD * N * PACK
+            for h in range(GROUP // W_LOAD):
+                nc.scalar.copy(
+                    out=w_bf[s][:, h * width:(h + 1) * width].rearrange("p (e c i j) -> p e c j i", e=W_LOAD, i=LINE, j=PACK),
+                    in_=w_raw[s, h][:].rearrange("p e (j c i) -> p e c j i", j=PACK, i=LINE))
 
-        def quantize(src, name):
-            codes = stage.tile([P, GROUP_SLOTS], U32, name=name + "_codes", align_bytes=64)
-            scales = stage.tile([P, GROUP_SLOTS], U8, name=name + "_scales", align_bytes=64)
+        def weave_x(s, e_lo, e_hi):
+            x_bf[s, e_lo] = stage.tile([P, (e_hi - e_lo) * C * PACK], BF16, name="x_bf", align_bytes=64)
+            nc.scalar.copy(out=x_bf[s, e_lo][:].rearrange("p (c i t) -> p c t i", i=LINE, t=PACK),
+                           in_=gathered[s, e_lo][:].rearrange("p t (c i) -> p c t i", i=LINE))
+
+        def quantize(src, width, name):
+            codes = stage.tile([P, width], U32, name=name + "_codes", align_bytes=64)
+            scales = stage.tile([P, width], U8, name=name + "_scales", align_bytes=64)
             nc.vector.quantize_mx(out=codes[:].bitcast(FP8X4), scales=scales[:], in_=src[:])
             return codes, scales
 
-        def multiply(s):
+        def multiply(s, e_lo, e_hi):
             c, g = steps[s]
-            w_codes, w_scales = quantize(w_bf[s], "w")
-            x_codes, x_scales = quantize(x_bf[s], "x")
-            for i in range(GROUP):
+            if e_lo == 0:
+                w_mx[s] = quantize(w_bf[s], GROUP * N, "w")
+            w_codes, w_scales = w_mx[s]
+            x_codes, x_scales = quantize(x_bf[s, e_lo], (e_hi - e_lo) * C, "x")
+            for i in range(e_lo, e_hi):
                 if g == 0:
                     banks[c, i] = psum.tile([N, C], F32, name="acc%d" % i)
-                cols = slice(i * C, (i + 1) * C)
-                nc.tensor.matmul_mx(out=banks[c, i][:], lhsT=w_codes[:, cols].bitcast(FP8X4), lhsT_scale=w_scales[:, cols],
-                                    rhs=x_codes[:, cols].bitcast(FP8X4), rhs_scale=x_scales[:, cols],
+                w_cols = slice(i * N, (i + 1) * N)
+                x_cols = slice((i - e_lo) * C, (i - e_lo + 1) * C)
+                nc.tensor.matmul_mx(out=banks[c, i][:], lhsT=w_codes[:, w_cols].bitcast(FP8X4), lhsT_scale=w_scales[:, w_cols],
+                                    rhs=x_codes[:, x_cols].bitcast(FP8X4), rhs_scale=x_scales[:, x_cols],
                                     start=(g == 0), stop=(g == PASSES - 1))
                 if g == PASSES - 1:
                     e = c * GROUP + i
@@ -100,30 +126,33 @@ def tile_moe_pre_lin_gelu_kernel(tc, xT, w, b, gate, offs, pos1, pos2, pos3, pos
 
         nc.sync.dma_start(slot_list[:], offs)
         load(0)
-        load(1)
         nc.sync.dma_start(out=bias[:], in_=b)
-        for tile, src in zip(pos_lists, (pos1, pos2, pos3, pos4)):
-            nc.sync.dma_start(tile[:], src)
         for s in range(len(steps) + 1):
-            if s + 2 < len(steps):
-                load(s + 2)
-            if s < len(steps):
-                gather(s)
-                weave(s)
+            if s + 1 <= last:
+                load(s + 1)
+            if s == PASSES:
+                for tile, src in zip(pos_lists, (pos1, pos2, pos3, pos4)):
+                    nc.sync.dma_start(tile[:], src)
+            if s <= last:
+                weave_w(s)
+                for piece in pieces(s):
+                    gather(s, *piece)
+                    weave_x(s, *piece)
             if s >= 1:
-                multiply(s - 1)
+                for piece in pieces(s - 1):
+                    multiply(s - 1, *piece)
 
         half = T // 2
         cols = half // PER_COL
-        sums = [None, None]
+        partial = [None, None]
         for r in range(TOP):
             for h in range(2):
                 picked = y[:].indirect(pos_lists[r][:, h * cols:(h + 1) * cols])
-                total = keep.tile([P, half], F32, name="sum%d_%d" % (r, h))
+                total = sums.tile([P, half], F32, name="total")
                 if r == 0:
                     nc.vector.tensor_copy(total[:], picked)
                 else:
-                    nc.vector.tensor_tensor(total[:], picked, sums[h][:], ADD)
-                sums[h] = total
-        nc.sync.dma_start(out=out[:, 0:half], in_=sums[0][:])
-        nc.scalar.dma_start(out=out[:, half:T], in_=sums[1][:])
+                    nc.vector.tensor_tensor(total[:], picked, partial[h][:], ADD)
+                partial[h] = total
+        nc.sync.dma_start(out=out[:, 0:half], in_=partial[0][:])
+        nc.scalar.dma_start(out=out[:, half:T], in_=partial[1][:])

@@ -60,7 +60,7 @@ def tile_moe_pre_lin_gelu_kernel(tc, xT, w, b, gate, offs, pos1, pos2, pos3, pos
         def load_gate(c, lo, hi):
             nc.sync.dma_start(out=gates[c][:, lo:hi], in_=gate[0:P, c * GROUP_SLOTS + lo:c * GROUP_SLOTS + hi])
 
-        def load(s):
+        def load_x(s):
             c, g = steps[s]
             if g == 0:
                 load_gate(c, 0, FIRST if s == 0 else GROUP_SLOTS)
@@ -69,6 +69,9 @@ def tile_moe_pre_lin_gelu_kernel(tc, xT, w, b, gate, offs, pos1, pos2, pos3, pos
                     nc.sync.dma_start(out=planes[g][t][:, 0:T], in_=x_rows[g, t])
                     if s == 0 and t == 0:
                         load_gate(c, FIRST, GROUP_SLOTS)
+
+        def load_w(s):
+            c, g = steps[s]
             for h in range(GROUP // W_LOAD):
                 e0 = c * GROUP + h * W_LOAD
                 w_raw[s, h] = wload.tile([P, W_LOAD, PACK * N], F32, name="w_raw")
@@ -76,16 +79,14 @@ def tile_moe_pre_lin_gelu_kernel(tc, xT, w, b, gate, offs, pos1, pos2, pos3, pos
                     out=w_raw[s, h][:],
                     in_=w[e0:e0 + W_LOAD, g * K_PASS:(g + 1) * K_PASS, :].rearrange("e (p j) n -> p e (j n)", j=PACK))
 
-        def gather(s, e_lo, e_hi):
+        def gather(s):
             c, g = steps[s]
-            tile = stage.tile([P, PACK, (e_hi - e_lo) * C], F32, name="gathered" if e_lo == 0 else "gathered_tail")
-            gathered[s, e_lo] = tile
+            gathered[s] = stage.tile([P, PACK, GROUP_SLOTS], F32, name="gathered")
             for t in range(PACK):
-                lo, hi = e_lo * C, e_hi * C
-                cuts = [lo, FIRST, hi] if s == 0 and t == 0 else [lo, hi]
+                cuts = [0, FIRST, GROUP_SLOTS] if s == 0 and t == 0 else [0, GROUP_SLOTS]
                 for a, z in zip(cuts, cuts[1:]):
                     offsets = slot_list[:, (c * GROUP_SLOTS + a) // PER_COL:(c * GROUP_SLOTS + z) // PER_COL]
-                    nc.vector.tensor_tensor(tile[:, t, a - lo:z - lo], planes[g][t][:].indirect(offsets), gates[c][:, a:z], MULT)
+                    nc.vector.tensor_tensor(gathered[s][:, t, a:z], planes[g][t][:].indirect(offsets), gates[c][:, a:z], MULT)
 
         def weave_w(s):
             w_bf[s] = stage.tile([P, GROUP * N * PACK], BF16, name="w_bf", align_bytes=64)
@@ -96,22 +97,25 @@ def tile_moe_pre_lin_gelu_kernel(tc, xT, w, b, gate, offs, pos1, pos2, pos3, pos
                     in_=w_raw[s, h][:].rearrange("p e (j c i) -> p e c j i", j=PACK, i=LINE))
 
         def weave_x(s, e_lo, e_hi):
-            x_bf[s, e_lo] = stage.tile([P, (e_hi - e_lo) * C * PACK], BF16, name="x_bf", align_bytes=64)
+            x_bf[s, e_lo] = stage.tile([P, (e_hi - e_lo) * C * PACK], BF16, name="x_bf", align_bytes=64, bufs=3)
             nc.scalar.copy(out=x_bf[s, e_lo][:].rearrange("p (c i t) -> p c t i", i=LINE, t=PACK),
-                           in_=gathered[s, e_lo][:].rearrange("p t (c i) -> p c t i", i=LINE))
+                           in_=gathered[s][:, :, e_lo * C:e_hi * C].rearrange("p t (c i) -> p c t i", i=LINE))
 
-        def quantize(src, width, name):
+        def quantize(src, width, call_width, name):
             codes = stage.tile([P, width], U32, name=name + "_codes", align_bytes=64)
             scales = stage.tile([P, width], U8, name=name + "_scales", align_bytes=64)
-            nc.vector.quantize_mx(out=codes[:].bitcast(FP8X4), scales=scales[:], in_=src[:])
+            for lo in range(0, width, call_width):
+                hi = lo + call_width
+                nc.vector.quantize_mx(out=codes[:, lo:hi].bitcast(FP8X4), scales=scales[:, lo:hi], in_=src[:, lo * PACK:hi * PACK])
             return codes, scales
 
         def multiply(s, e_lo, e_hi):
             c, g = steps[s]
             if e_lo == 0:
-                w_mx[s] = quantize(w_bf[s], GROUP * N, "w")
+                w_mx[s] = quantize(w_bf[s], GROUP * N, GROUP * N, "w")
             w_codes, w_scales = w_mx[s]
-            x_codes, x_scales = quantize(x_bf[s, e_lo], (e_hi - e_lo) * C, "x")
+            width = (e_hi - e_lo) * C
+            x_codes, x_scales = quantize(x_bf[s, e_lo], width, C if e_lo > 0 else width, "x")
             for i in range(e_lo, e_hi):
                 if g == 0:
                     banks[c, i] = psum.tile([N, C], F32, name="acc%d" % i)
@@ -125,18 +129,20 @@ def tile_moe_pre_lin_gelu_kernel(tc, xT, w, b, gate, offs, pos1, pos2, pos3, pos
                     nc.scalar.activation(out=y[:, e * C:(e + 1) * C], in_=banks[c, i][:], func=GELU, bias=bias[:, e:e + 1])
 
         nc.sync.dma_start(slot_list[:], offs)
-        load(0)
-        nc.sync.dma_start(out=bias[:], in_=b)
+        load_x(0)
         for s in range(len(steps) + 1):
             if s + 1 <= last:
-                load(s + 1)
-            if s == PASSES:
+                load_x(s + 1)
+            if s <= last:
+                load_w(s)
+            if s == PASSES - 1:
+                nc.sync.dma_start(out=bias[:], in_=b)
                 for tile, src in zip(pos_lists, (pos1, pos2, pos3, pos4)):
                     nc.sync.dma_start(tile[:], src)
             if s <= last:
+                gather(s)
                 weave_w(s)
                 for piece in pieces(s):
-                    gather(s, *piece)
                     weave_x(s, *piece)
             if s >= 1:
                 for piece in pieces(s - 1):

@@ -81,12 +81,16 @@ def tile_moe_pre_lin_gelu_kernel(tc, xT, w, b, gate, offs, pos1, pos2, pos3, pos
 
         def gather(s):
             c, g = steps[s]
-            gathered[s] = stage.tile([P, PACK, GROUP_SLOTS], F32, name="gathered")
-            for t in range(PACK):
-                cuts = [0, FIRST, GROUP_SLOTS] if s == 0 and t == 0 else [0, GROUP_SLOTS]
-                for a, z in zip(cuts, cuts[1:]):
-                    offsets = slot_list[:, (c * GROUP_SLOTS + a) // PER_COL:(c * GROUP_SLOTS + z) // PER_COL]
-                    nc.vector.tensor_tensor(gathered[s][:, t, a:z], planes[g][t][:].indirect(offsets), gates[c][:, a:z], MULT)
+            tile = stage.tile([P, PACK * GROUP_SLOTS], F32, name="gathered")
+            for e_lo, e_hi in pieces(s):
+                lo, hi = e_lo * C, e_hi * C
+                gathered[s, e_lo] = tile[:, lo * PACK:hi * PACK].rearrange("p (t m) -> p t m", t=PACK)
+                for t in range(PACK):
+                    cuts = [lo, FIRST, hi] if s == 0 and t == 0 else [lo, hi]
+                    for a, z in zip(cuts, cuts[1:]):
+                        offsets = slot_list[:, (c * GROUP_SLOTS + a) // PER_COL:(c * GROUP_SLOTS + z) // PER_COL]
+                        nc.vector.tensor_tensor(gathered[s, e_lo][:, t, a - lo:z - lo], planes[g][t][:].indirect(offsets),
+                                                gates[c][:, a:z], MULT)
 
         def weave_w(s):
             w_bf[s] = stage.tile([P, GROUP * N * PACK], BF16, name="w_bf", align_bytes=64)
@@ -99,7 +103,7 @@ def tile_moe_pre_lin_gelu_kernel(tc, xT, w, b, gate, offs, pos1, pos2, pos3, pos
         def weave_x(s, e_lo, e_hi):
             x_bf[s, e_lo] = stage.tile([P, (e_hi - e_lo) * C * PACK], BF16, name="x_bf", align_bytes=64, bufs=3)
             nc.scalar.copy(out=x_bf[s, e_lo][:].rearrange("p (c i t) -> p c t i", i=LINE, t=PACK),
-                           in_=gathered[s][:, :, e_lo * C:e_hi * C].rearrange("p t (c i) -> p c t i", i=LINE))
+                           in_=gathered[s, e_lo].rearrange("p t (c i) -> p c t i", i=LINE))
 
         def quantize(src, width, call_width, name):
             codes = stage.tile([P, width], U32, name=name + "_codes", align_bytes=64)

from contextlib import ExitStack

import concourse.mybir as mybir

K, T, E, C, N = 2048, 768, 24, 128, 128
TOP = 4
SLOTS = E * C
FLOPS = 2 * K * N * SLOTS
BYTES = 4 * (K * T + E * K * N + N * E + SLOTS + N * T) + 2 * 128 * (SLOTS + TOP * T) // 16

F32 = mybir.dt.float32
BF16 = mybir.dt.bfloat16
U32 = mybir.dt.uint32
U16 = mybir.dt.uint16
U8 = mybir.dt.uint8
FP8X4 = mybir.dt.float8_e4m3fn_x4
MULT = mybir.AluOpType.mult
ADD = mybir.AluOpType.add
GELU = mybir.ActivationFunctionType.Gelu_apprx_tanh

P = 128
PACK = 4
K_PASS = P * PACK
PASSES = K // K_PASS
GROUP = 8
GROUP_SLOTS = GROUP * C
GROUPS = E // GROUP
PER_COL = 16
WINDOW = GROUP_SLOTS + PER_COL
LINE = 4
W_LOAD = 4
FIRST = 256


def tile_moe_pre_lin_gelu_kernel(tc, xT, w, b, gate, offs, pos1, pos2, pos3, pos4, out):
    nc = tc.nc
    steps = [(c, g) for c in range(GROUPS) for g in range(PASSES)]
    last = len(steps) - 1
    x_rows = xT.rearrange("(g p t) s -> g t p s", p=P, t=PACK)

    with ExitStack() as ctx:
        keep = ctx.enter_context(tc.tile_pool(name="keep", bufs=1))
        wload = ctx.enter_context(tc.tile_pool(name="wload", bufs=4))
        stage = ctx.enter_context(tc.tile_pool(name="stage", bufs=2))
        sums = ctx.enter_context(tc.tile_pool(name="sums", bufs=4))
        psum = ctx.enter_context(tc.psum_pool(name="psum", bufs=1))

        slot_list = keep.tile([P, SLOTS // PER_COL], U16, name="slot_list")
        pos_lists = [keep.tile([P, T // PER_COL], U16, name="pos_list%d" % r) for r in range(TOP)]
        planes = [[keep.tile([P, WINDOW], F32, name="plane%d_%d" % (g, t)) for t in range(PACK)] for g in range(PASSES)]
        gates = [keep.tile([P, GROUP_SLOTS], F32, name="gate%d" % c) for c in range(GROUPS)]
        bias = keep.tile([P, E], F32, name="bias")
        y = keep.tile([P, SLOTS], F32, name="y")

        w_raw, w_bf, w_mx, gathered, x_bf, banks = {}, {}, {}, {}, {}, {}

        def pieces(s):
            return [(0, GROUP)] if s < last else [(0, GROUP // 2), (GROUP // 2, GROUP)]

        def load_gate(c, lo, hi):
            nc.sync.dma_start(out=gates[c][:, lo:hi], in_=gate[0:P, c * GROUP_SLOTS + lo:c * GROUP_SLOTS + hi])

        def load_x(s):
            c, g = steps[s]
            if g == 0:
                load_gate(c, 0, FIRST if s == 0 else GROUP_SLOTS)
            if c == 0:
                for t in range(PACK):
                    nc.sync.dma_start(out=planes[g][t][:, 0:T], in_=x_rows[g, t])
                    if s == 0 and t == 0:
                        load_gate(c, FIRST, GROUP_SLOTS)

        def load_w(s):
            c, g = steps[s]
            for h in range(GROUP // W_LOAD):
                e0 = c * GROUP + h * W_LOAD
                w_raw[s, h] = wload.tile([P, W_LOAD, PACK * N], F32, name="w_raw")
                nc.sync.dma_start(
                    out=w_raw[s, h][:],
                    in_=w[e0:e0 + W_LOAD, g * K_PASS:(g + 1) * K_PASS, :].rearrange("e (p j) n -> p e (j n)", j=PACK))

        def gather(s):
            c, g = steps[s]
            tile = stage.tile([P, PACK * GROUP_SLOTS], F32, name="gathered")
            for e_lo, e_hi in pieces(s):
                lo, hi = e_lo * C, e_hi * C
                gathered[s, e_lo] = tile[:, lo * PACK:hi * PACK].rearrange("p (t m) -> p t m", t=PACK)
                for t in range(PACK):
                    cuts = [lo, FIRST, hi] if s == 0 and t == 0 else [lo, hi]
                    for a, z in zip(cuts, cuts[1:]):
                        offsets = slot_list[:, (c * GROUP_SLOTS + a) // PER_COL:(c * GROUP_SLOTS + z) // PER_COL]
                        nc.vector.tensor_tensor(gathered[s, e_lo][:, t, a - lo:z - lo], planes[g][t][:].indirect(offsets),
                                                gates[c][:, a:z], MULT)

        def weave_w(s):
            w_bf[s] = stage.tile([P, GROUP * N * PACK], BF16, name="w_bf", align_bytes=64)
            width = W_LOAD * N * PACK
            for h in range(GROUP // W_LOAD):
                nc.scalar.copy(
                    out=w_bf[s][:, h * width:(h + 1) * width].rearrange("p (e c i j) -> p e c j i", e=W_LOAD, i=LINE, j=PACK),
                    in_=w_raw[s, h][:].rearrange("p e (j c i) -> p e c j i", j=PACK, i=LINE))

        def weave_x(s, e_lo, e_hi):
            x_bf[s, e_lo] = stage.tile([P, (e_hi - e_lo) * C * PACK], BF16, name="x_bf", align_bytes=64, bufs=3)
            nc.scalar.copy(out=x_bf[s, e_lo][:].rearrange("p (c i t) -> p c t i", i=LINE, t=PACK),
                           in_=gathered[s, e_lo].rearrange("p t (c i) -> p c t i", i=LINE))

        def quantize(src, width, call_width, name):
            codes = stage.tile([P, width], U32, name=name + "_codes", align_bytes=64)
            scales = stage.tile([P, width], U8, name=name + "_scales", align_bytes=64)
            for lo in range(0, width, call_width):
                hi = lo + call_width
                nc.vector.quantize_mx(out=codes[:, lo:hi].bitcast(FP8X4), scales=scales[:, lo:hi], in_=src[:, lo * PACK:hi * PACK])
            return codes, scales

        def multiply(s, e_lo, e_hi):
            c, g = steps[s]
            if e_lo == 0:
                w_mx[s] = quantize(w_bf[s], GROUP * N, GROUP * N, "w")
            w_codes, w_scales = w_mx[s]
            width = (e_hi - e_lo) * C
            x_codes, x_scales = quantize(x_bf[s, e_lo], width, C if e_lo > 0 else width, "x")
            for i in range(e_lo, e_hi):
                if g == 0:
                    banks[c, i] = psum.tile([N, C], F32, name="acc%d" % i)
                w_cols = slice(i * N, (i + 1) * N)
                x_cols = slice((i - e_lo) * C, (i - e_lo + 1) * C)
                nc.tensor.matmul_mx(out=banks[c, i][:], lhsT=w_codes[:, w_cols].bitcast(FP8X4), lhsT_scale=w_scales[:, w_cols],
                                    rhs=x_codes[:, x_cols].bitcast(FP8X4), rhs_scale=x_scales[:, x_cols],
                                    start=(g == 0), stop=(g == PASSES - 1))
                if g == PASSES - 1:
                    e = c * GROUP + i
                    nc.scalar.activation(out=y[:, e * C:(e + 1) * C], in_=banks[c, i][:], func=GELU, bias=bias[:, e:e + 1])

        nc.sync.dma_start(slot_list[:], offs)
        load_x(0)
        for s in range(len(steps) + 1):
            if s + 1 <= last:
                load_x(s + 1)
            if s <= last:
                load_w(s)
            if s == PASSES - 1:
                nc.sync.dma_start(out=bias[:], in_=b)
                for tile, src in zip(pos_lists, (pos1, pos2, pos3, pos4)):
                    nc.sync.dma_start(tile[:], src)
            if s <= last:
                gather(s)
                weave_w(s)
                for piece in pieces(s):
                    weave_x(s, *piece)
            if s >= 1:
                for piece in pieces(s - 1):
                    multiply(s - 1, *piece)

        half = T // 2
        cols = half // PER_COL
        partial = [None, None]
        for r in range(TOP):
            for h in range(2):
                picked = y[:].indirect(pos_lists[r][:, h * cols:(h + 1) * cols])
                total = sums.tile([P, half], F32, name="total")
                if r == 0:
                    nc.vector.tensor_copy(total[:], picked)
                else:
                    nc.vector.tensor_tensor(total[:], picked, partial[h][:], ADD)
                partial[h] = total
        nc.sync.dma_start(out=out[:, 0:half], in_=partial[0][:])
        nc.scalar.dma_start(out=out[:, half:T], in_=partial[1][:])
